import numpy as np
import ml_dtypes


def mxq(x, axis, fmt="e4m3"):
    dtype, down = {"e4m3": (ml_dtypes.float8_e4m3fn, 7), "e5m2": (ml_dtypes.float8_e5m2, 14)}[fmt]
    v = np.moveaxis(np.asarray(x, np.float32).astype(ml_dtypes.bfloat16).astype(np.float64), axis, -1)
    blocks = v.reshape(v.shape[:-1] + (-1, 32))
    amax = np.abs(blocks).max(-1, keepdims=True)
    byte = np.maximum(np.where(amax > 0, np.frexp(amax)[1] - 1 + 127, 0) - down, 1)
    scale = np.exp2(byte - 127.0)
    codes = (blocks / scale).astype(np.float32).astype(dtype).astype(np.float64)
    return np.moveaxis((codes * scale).reshape(v.shape), -1, axis)


WIDE = False


def mx_kscale(k):
    if not WIDE:
        return np.ones(k)
    levels = np.array([10, -10, 5, -5, 0])
    if k % 512:
        return np.exp2(np.random.permutation(np.resize(levels, k // 32))).repeat(32)
    a = np.empty((k // 512, 16))
    for p in range(k // 512):
        a[p, :8] = np.random.permutation(np.resize(levels, 8))
        for g in range(8):
            far = levels[np.abs(levels - a[p, g]) >= 10]
            a[p, g + 8] = far[np.random.randint(len(far))]
    return np.exp2(a.ravel()).repeat(32)


def f64(x):
    return np.asarray(x).astype(np.float64)


def striped(idx):
    return np.tile(idx.reshape(-1, 16).T, (8, 1)).astype(np.uint16)


def unstriped(offs):
    return offs[:16].T.reshape(-1).astype(np.int64)


def pack_weight(w):
    k, n = w.shape
    w = f64(np.asarray(w, np.float32).astype(ml_dtypes.bfloat16)).reshape(k // 32, 32, n)
    amax = np.abs(w).max(1)
    byte = np.clip(np.where(amax > 0, np.frexp(amax)[1] - 1 + 127 - 7, 1), 1, 254)
    scaled = (w * np.exp2(127.0 - byte)[:, None, :]).reshape(k, n).astype(np.float32)
    words = np.ascontiguousarray(scaled.reshape(k // 512, 128, 4, n).transpose(0, 1, 3, 2)).astype(ml_dtypes.float8_e4m3fn).view(np.uint8)
    return words, np.ascontiguousarray(byte.astype(np.uint8).reshape(k // 512, 16, n))


def unpack_weight(words, scales):
    g, p, n, _ = words.shape
    vals = np.ascontiguousarray(words).view(ml_dtypes.float8_e4m3fn).astype(np.float64) * np.repeat(np.exp2(scales.astype(np.float64) - 127.0), 8, axis=1)[..., None]
    return vals.transpose(0, 1, 3, 2).reshape(g * 512, n)


def relu(v):
    return np.maximum(v, 0.0)


K, T, S, H, N = 1024, 2048, 1024, 512, 128


def setup_inputs():
    n = np.random.standard_normal
    s = mx_kscale(K)[:, None]
    u = mx_kscale(H)
    packed = pack_weight(n((K, T)) * s)
    return {
        "x_words": packed[0],
        "x_scales": packed[1],
        "w1": (n((K, H)) / np.sqrt(K) / s * u).astype(np.float32),
        "w2": (n((H, N)) / np.sqrt(H) / u[:, None]).astype(np.float32),
        "gate": np.tile(np.random.uniform(0.2, 1.0, S), (N, 1)).astype(np.float32),
        "offs": striped(np.sort(np.random.permutation(T)[:S])),
    }


def reference(x_words, x_scales, w1, w2, gate, offs):
    idx = unstriped(offs)
    xq = unpack_weight(x_words, x_scales)[:, idx]
    h = relu(mxq(f64(w1), 0, "e4m3").T @ xq)
    y = mxq(f64(w2), 0, "e4m3").T @ mxq(h, 0, "e4m3")
    out = np.zeros((N, T))
    out[:, idx] = f64(gate) * y
    return out

@@ -1,0 +1,201 @@
+from contextlib import ExitStack
+
+import concourse.mybir as mybir
+
+K, T, S, H, N = 1024, 2048, 1024, 512, 128
+FLOPS = 2 * K * H * S + 2 * H * N * S
+
+F32 = mybir.dt.float32
+BF16 = mybir.dt.bfloat16
+I32 = mybir.dt.int32
+U32 = mybir.dt.uint32
+U16 = mybir.dt.uint16
+U8 = mybir.dt.uint8
+FP8X4 = mybir.dt.float8_e4m3fn_x4
+RELU = mybir.ActivationFunctionType.Relu
+MULT = mybir.AluOpType.mult
+
+P = 128
+PACK = 4
+PASSES = K // (P * PACK)
+BLOCK = 128
+SLICE = 256
+BLOCKS = S // BLOCK
+SLICES = S // SLICE
+PER_COL = 16
+
+
+def tile_picked_depth_mlp_relu_srt_p_kernel(
+    tc, x_words, x_scales, w1, w2, gate, offs, out
+):
+    nc = tc.nc
+    with ExitStack() as ctx:
+        keep = ctx.enter_context(tc.tile_pool(name="keep", bufs=1))
+        psum = ctx.enter_context(tc.psum_pool(name="psum", bufs=1))
+
+        offsets = keep.tile([P, S // PER_COL], U16, name="offsets")
+        nc.sync.dma_start(offsets[:], offs)
+
+        def entries(first, count):
+            return offsets[:, first // PER_COL : (first + count) // PER_COL]
+
+        scale_window = keep.tile([P, T], U8, name="scale_window", align_bytes=64)
+        nc.vector.memset(scale_window[:].bitcast(I32), 0)
+        scale_rows = x_scales.bitcast(I32)
+        scale_stage = keep.tile([P, T // 4], I32, name="scale_stage")
+        for quad in range(4):
+            live = slice(32 * quad, 32 * quad + 8)
+            nc.scalar.dma_start(scale_stage[live, :], scale_rows[:, 4 * quad : 4 * quad + 4, :])
+            nc.vector.tensor_copy(scale_window[live, :].bitcast(I32), scale_stage[live, :])
+        out_window = keep.tile([P, T], F32, name="out_window")
+        nc.vector.memset(out_window[:], 0.0)
+
+        word_window = [keep.tile([P, T], I32, name="word_window%d" % o) for o in range(PASSES)]
+
+        def load_words(o, first, last):
+            src = x_words[o].rearrange("p n t -> p (n t)")[:, PACK * first : PACK * last]
+            nc.sync.dma_start(word_window[o][:, first:last], src.bitcast(I32))
+
+        w1_raw = {}
+
+        def load_w1(o, half):
+            raw = keep.tile([P, PACK, H // 2], F32, name="w1_raw%d%d" % (o, half))
+            rows = w1[512 * o : 512 * (o + 1), (H // 2) * half : (H // 2) * (half + 1)]
+            nc.sync.dma_start(raw[:], rows.rearrange("(p j) c -> p j c", j=PACK))
+            w1_raw[o, half] = raw
+
+        load_words(0, 0, T)
+        for o in range(PASSES):
+            for half in range(2):
+                load_w1(o, half)
+        reach = [T - S + SLICE * (s + 1) for s in range(SLICES)]
+        load_words(1, 0, reach[0])
+        load_words(1, reach[0], reach[1])
+        w2_raw = keep.tile([P, PACK, N], F32, name="w2_raw")
+        nc.sync.dma_start(w2_raw[:], w2.rearrange("(p j) n -> p j n", j=PACK))
+        load_words(1, reach[1], reach[2])
+        load_words(1, reach[2], reach[3])
+        gate_sb = [keep.tile([P, S // 2], F32, name="gate_sb%d" % g) for g in range(2)]
+        for g in range(2):
+            nc.sync.dma_start(gate_sb[g][:], gate[:, (S // 2) * g : (S // 2) * (g + 1)])
+
+        picked_scales = keep.tile([P, S], U8, name="picked_scales", align_bytes=64)
+        nc.vector.tensor_copy(picked_scales[:], scale_window[:].indirect(offsets[:]))
+        picked0 = [keep.tile([P, S // 2], U32, name="picked0_%d" % g, align_bytes=64) for g in range(2)]
+        for g in range(2):
+            nc.vector.tensor_copy(
+                picked0[g][:], word_window[0][:].bitcast(U32).indirect(entries((S // 2) * g, S // 2))
+            )
+
+        w1_bf = [keep.tile([P, PACK, P, PACK], BF16, name="w1_bf%d" % o, align_bytes=64) for o in range(PASSES)]
+        w1_codes = [keep.tile([P, H], U32, name="w1_codes%d" % o, align_bytes=64) for o in range(PASSES)]
+        w1_scales = [keep.tile([P, H], U8, name="w1_scales%d" % o, align_bytes=64) for o in range(PASSES)]
+
+        def round_w1(o, half, copy):
+            dst = w1_bf[o][:, :, 64 * half : 64 * (half + 1), :].rearrange("p t m j -> p m j t")
+            copy(dst, w1_raw[o, half][:].rearrange("p j (m t) -> p m j t", t=PACK))
+
+        def quantise_w1(o):
+            nc.vector.quantize_mx(
+                out=w1_codes[o][:].bitcast(FP8X4),
+                scales=w1_scales[o][:],
+                in_=w1_bf[o][:].rearrange("p t m j -> p (t m j)"),
+            )
+
+        round_w1(0, 0, nc.scalar.copy)
+        round_w1(0, 1, nc.scalar.copy)
+        quantise_w1(0)
+        round_w1(1, 0, nc.scalar.copy)
+        round_w1(1, 1, nc.vector.tensor_copy)
+        quantise_w1(1)
+
+        banks = [psum.tile([P, PACK, BLOCK], F32, name="bank%d" % b, tag="bank%d" % b) for b in range(BLOCKS)]
+        picked1 = [keep.tile([P, SLICE], U32, name="picked1_%d" % s, align_bytes=64) for s in range(SLICES)]
+
+        def first_layer(o, b):
+            if o == 0:
+                words = picked0[b // 4][:, BLOCK * (b % 4) : BLOCK * (b % 4 + 1)]
+            else:
+                words = picked1[b // 2][:, BLOCK * (b % 2) : BLOCK * (b % 2 + 1)]
+            for t in range(PACK):
+                nc.tensor.matmul_mx(
+                    out=banks[b][:, t, :],
+                    lhsT=w1_codes[o][:, P * t : P * (t + 1)].bitcast(FP8X4),
+                    lhsT_scale=w1_scales[o][:, P * t : P * (t + 1)],
+                    rhs=words.bitcast(FP8X4),
+                    rhs_scale=picked_scales[4 * o : P, BLOCK * b : BLOCK * (b + 1)],
+                    start=(o == 0 and t == 0),
+                    stop=(o == PASSES - 1 and t == PACK - 1),
+                )
+
+        for b in range(BLOCKS):
+            first_layer(0, b)
+
+        w2_bf = keep.tile([P, N, PACK], BF16, name="w2_bf", align_bytes=64)
+        w2_codes = keep.tile([P, N], U32, name="w2_codes", align_bytes=64)
+        w2_scales = keep.tile([P, N], U8, name="w2_scales", align_bytes=64)
+
+        h_bf = [keep.tile([P, SLICE, PACK], BF16, name="h_bf%d" % s, align_bytes=64) for s in range(SLICES)]
+        h_codes = [keep.tile([P, SLICE], U32, name="h_codes%d" % s, align_bytes=64) for s in range(SLICES)]
+        h_scales = [keep.tile([P, SLICE], U8, name="h_scales%d" % s, align_bytes=64) for s in range(SLICES)]
+        y_sb = [keep.tile([P, SLICE], F32, name="y_sb%d" % s) for s in range(SLICES)]
+
+        def hidden(s):
+            nc.vector.tensor_copy(
+                picked1[s][:], word_window[1][:, 0 : reach[s]].bitcast(U32).indirect(entries(SLICE * s, SLICE))
+            )
+            for b in (2 * s, 2 * s + 1):
+                first_layer(1, b)
+                nc.scalar.activation(
+                    h_bf[s][:, BLOCK * (b % 2) : BLOCK * (b % 2 + 1), :],
+                    banks[b][:].rearrange("p t n -> p n t"),
+                    RELU,
+                )
+
+        def second_layer(s):
+            nc.vector.quantize_mx(
+                out=h_codes[s][:].bitcast(FP8X4),
+                scales=h_scales[s][:],
+                in_=h_bf[s][:].rearrange("p n t -> p (n t)"),
+            )
+            y_bank = psum.tile([P, SLICE], F32, name="y_bank%d" % s, tag="bank%d" % (2 * s))
+            nc.tensor.matmul_mx(
+                out=y_bank[:],
+                lhsT=w2_codes[:].bitcast(FP8X4),
+                lhsT_scale=w2_scales[:],
+                rhs=h_codes[s][:].bitcast(FP8X4),
+                rhs_scale=h_scales[s][:],
+                start=True,
+                stop=True,
+            )
+            nc.scalar.copy(y_sb[s][:], y_bank[:])
+
+        def put_back(s):
+            nc.vector.tensor_tensor(
+                out_window[:].indirect(entries(SLICE * s, SLICE)),
+                y_sb[s][:],
+                gate_sb[s // 2][:, SLICE * (s % 2) : SLICE * (s % 2 + 1)],
+                MULT,
+            )
+
+        hidden(0)
+        hidden(1)
+        nc.vector.tensor_copy(
+            w2_bf[:].rearrange("p (c i) j -> p c j i", i=PACK),
+            w2_raw[:].rearrange("p j (c i) -> p c j i", i=PACK),
+        )
+        hidden(2)
+        nc.vector.quantize_mx(
+            out=w2_codes[:].bitcast(FP8X4),
+            scales=w2_scales[:],
+            in_=w2_bf[:].rearrange("p n j -> p (n j)"),
+        )
+        second_layer(0)
+        hidden(3)
+        for s in range(1, SLICES):
+            second_layer(s)
+            put_back(s - 1)
+        put_back(SLICES - 1)
+
+        nc.sync.dma_start(out[:, 0 : T // 2], out_window[:, 0 : T // 2])
+        nc.scalar.dma_start(out[:, T // 2 : T], out_window[:, T // 2 : T])

@@ -34,7 +34,6 @@ def tile_picked_depth_mlp_relu_srt_p_kernel(
         psum = ctx.enter_context(tc.psum_pool(name="psum", bufs=1))
 
         offsets = keep.tile([P, S // PER_COL], U16, name="offsets")
-        nc.sync.dma_start(offsets[:], offs)
 
         def entries(first, count):
             return offsets[:, first // PER_COL : (first + count) // PER_COL]
@@ -45,8 +44,9 @@ def tile_picked_depth_mlp_relu_srt_p_kernel(
         scale_stage = keep.tile([P, T // 4], I32, name="scale_stage")
         for quad in range(4):
             live = slice(32 * quad, 32 * quad + 8)
-            nc.scalar.dma_start(scale_stage[live, :], scale_rows[:, 4 * quad : 4 * quad + 4, :])
+            nc.sync.dma_start(scale_stage[live, :], scale_rows[:, 4 * quad : 4 * quad + 4, :])
             nc.vector.tensor_copy(scale_window[live, :].bitcast(I32), scale_stage[live, :])
+        nc.sync.dma_start(offsets[:], offs)
         out_window = keep.tile([P, T], F32, name="out_window")
         nc.vector.memset(out_window[:], 0.0)
 
@@ -64,11 +64,13 @@ def tile_picked_depth_mlp_relu_srt_p_kernel(
             nc.sync.dma_start(raw[:], rows.rearrange("(p j) c -> p j c", j=PACK))
             w1_raw[o, half] = raw
 
-        load_words(0, 0, T)
-        for o in range(PASSES):
-            for half in range(2):
-                load_w1(o, half)
         reach = [T - S + SLICE * (s + 1) for s in range(SLICES)]
+        load_w1(0, 0)
+        load_w1(0, 1)
+        load_words(0, 0, reach[1])
+        load_words(0, reach[1], T)
+        load_w1(1, 0)
+        load_w1(1, 1)
         load_words(1, 0, reach[0])
         load_words(1, reach[0], reach[1])
         w2_raw = keep.tile([P, PACK, N], F32, name="w2_raw")
@@ -82,18 +84,19 @@ def tile_picked_depth_mlp_relu_srt_p_kernel(
         picked_scales = keep.tile([P, S], U8, name="picked_scales", align_bytes=64)
         nc.vector.tensor_copy(picked_scales[:], scale_window[:].indirect(offsets[:]))
         picked0 = [keep.tile([P, S // 2], U32, name="picked0_%d" % g, align_bytes=64) for g in range(2)]
-        for g in range(2):
-            nc.vector.tensor_copy(
-                picked0[g][:], word_window[0][:].bitcast(U32).indirect(entries((S // 2) * g, S // 2))
-            )
+
+        def pick0(g):
+            window = word_window[0][:, 0 : reach[2 * g + 1]].bitcast(U32)
+            nc.vector.tensor_copy(picked0[g][:], window.indirect(entries((S // 2) * g, S // 2)))
 
         w1_bf = [keep.tile([P, PACK, P, PACK], BF16, name="w1_bf%d" % o, align_bytes=64) for o in range(PASSES)]
         w1_codes = [keep.tile([P, H], U32, name="w1_codes%d" % o, align_bytes=64) for o in range(PASSES)]
         w1_scales = [keep.tile([P, H], U8, name="w1_scales%d" % o, align_bytes=64) for o in range(PASSES)]
 
-        def round_w1(o, half, copy):
-            dst = w1_bf[o][:, :, 64 * half : 64 * (half + 1), :].rearrange("p t m j -> p m j t")
-            copy(dst, w1_raw[o, half][:].rearrange("p j (m t) -> p m j t", t=PACK))
+        def round_w1(o, half, copy, first=0, last=64):
+            dst = w1_bf[o][:, :, 64 * half + first : 64 * half + last, :].rearrange("p t m j -> p m j t")
+            src = w1_raw[o, half][:, :, PACK * first : PACK * last]
+            copy(dst, src.rearrange("p j (m t) -> p m j t", t=PACK))
 
         def quantise_w1(o):
             nc.vector.quantize_mx(
@@ -105,11 +108,14 @@ def tile_picked_depth_mlp_relu_srt_p_kernel(
         round_w1(0, 0, nc.scalar.copy)
         round_w1(0, 1, nc.scalar.copy)
         quantise_w1(0)
+        pick0(0)
+        pick0(1)
         round_w1(1, 0, nc.scalar.copy)
-        round_w1(1, 1, nc.vector.tensor_copy)
+        round_w1(1, 1, nc.scalar.copy, 0, 24)
+        round_w1(1, 1, nc.vector.tensor_copy, 24, 64)
         quantise_w1(1)
 
-        banks = [psum.tile([P, PACK, BLOCK], F32, name="bank%d" % b, tag="bank%d" % b) for b in range(BLOCKS)]
+        banks = {}
         picked1 = [keep.tile([P, SLICE], U32, name="picked1_%d" % s, align_bytes=64) for s in range(SLICES)]
 
         def first_layer(o, b):
@@ -128,9 +134,6 @@ def tile_picked_depth_mlp_relu_srt_p_kernel(
                     stop=(o == PASSES - 1 and t == PACK - 1),
                 )
 
-        for b in range(BLOCKS):
-            first_layer(0, b)
-
         w2_bf = keep.tile([P, N, PACK], BF16, name="w2_bf", align_bytes=64)
         w2_codes = keep.tile([P, N], U32, name="w2_codes", align_bytes=64)
         w2_scales = keep.tile([P, N], U8, name="w2_scales", align_bytes=64)
@@ -145,6 +148,8 @@ def tile_picked_depth_mlp_relu_srt_p_kernel(
                 picked1[s][:], word_window[1][:, 0 : reach[s]].bitcast(U32).indirect(entries(SLICE * s, SLICE))
             )
             for b in (2 * s, 2 * s + 1):
+                banks[b] = psum.tile([P, PACK, BLOCK], F32, name="bank%d" % b, tag="bank%d" % (b % 4))
+                first_layer(0, b)
                 first_layer(1, b)
                 nc.scalar.activation(
                     h_bf[s][:, BLOCK * (b % 2) : BLOCK * (b % 2 + 1), :],
@@ -158,7 +163,7 @@ def tile_picked_depth_mlp_relu_srt_p_kernel(
                 scales=h_scales[s][:],
                 in_=h_bf[s][:].rearrange("p n t -> p (n t)"),
             )
-            y_bank = psum.tile([P, SLICE], F32, name="y_bank%d" % s, tag="bank%d" % (2 * s))
+            y_bank = psum.tile([P, SLICE], F32, name="y_bank%d" % s, tag="y_bank%d" % s)
             nc.tensor.matmul_mx(
                 out=y_bank[:],
                 lhsT=w2_codes[:].bitcast(FP8X4),
@@ -180,7 +185,7 @@ def tile_picked_depth_mlp_relu_srt_p_kernel(
 
         hidden(0)
         hidden(1)
-        nc.vector.tensor_copy(
+        nc.scalar.copy(
             w2_bf[:].rearrange("p (c i) j -> p c j i", i=PACK),
             w2_raw[:].rearrange("p j (c i) -> p c j i", i=PACK),
         )

@@ -23,6 +23,7 @@ SLICE = 256
 BLOCKS = S // BLOCK
 SLICES = S // SLICE
 PER_COL = 16
+VECTOR_RELU = (1,)
 
 
 def tile_picked_depth_mlp_relu_srt_p_kernel(
@@ -41,14 +42,12 @@ def tile_picked_depth_mlp_relu_srt_p_kernel(
         scale_window = keep.tile([P, T], U8, name="scale_window", align_bytes=64)
         nc.vector.memset(scale_window[:].bitcast(I32), 0)
         scale_rows = x_scales.bitcast(I32)
-        scale_stage = keep.tile([P, T // 4], I32, name="scale_stage")
+        nc.sync.dma_start(offsets[:], offs)
         for quad in range(4):
             live = slice(32 * quad, 32 * quad + 8)
-            nc.sync.dma_start(scale_stage[live, :], scale_rows[:, 4 * quad : 4 * quad + 4, :])
-            nc.vector.tensor_copy(scale_window[live, :].bitcast(I32), scale_stage[live, :])
-        nc.sync.dma_start(offsets[:], offs)
+            nc.sync.dma_start(scale_window[live, :].bitcast(I32), scale_rows[:, 4 * quad : 4 * quad + 4, :])
         out_window = keep.tile([P, T], F32, name="out_window")
-        nc.vector.memset(out_window[:], 0.0)
+        nc.vector.memset(out_window[:].bitcast(I32), 0)
 
         word_window = [keep.tile([P, T], I32, name="word_window%d" % o) for o in range(PASSES)]
 
@@ -72,9 +71,9 @@ def tile_picked_depth_mlp_relu_srt_p_kernel(
         load_w1(1, 0)
         load_w1(1, 1)
         load_words(1, 0, reach[0])
-        load_words(1, reach[0], reach[1])
         w2_raw = keep.tile([P, PACK, N], F32, name="w2_raw")
         nc.sync.dma_start(w2_raw[:], w2.rearrange("(p j) n -> p j n", j=PACK))
+        load_words(1, reach[0], reach[1])
         load_words(1, reach[1], reach[2])
         load_words(1, reach[2], reach[3])
         gate_sb = [keep.tile([P, S // 2], F32, name="gate_sb%d" % g) for g in range(2)]
@@ -151,11 +150,12 @@ def tile_picked_depth_mlp_relu_srt_p_kernel(
                 banks[b] = psum.tile([P, PACK, BLOCK], F32, name="bank%d" % b, tag="bank%d" % (b % 4))
                 first_layer(0, b)
                 first_layer(1, b)
-                nc.scalar.activation(
-                    h_bf[s][:, BLOCK * (b % 2) : BLOCK * (b % 2 + 1), :],
-                    banks[b][:].rearrange("p t n -> p n t"),
-                    RELU,
-                )
+                dst = h_bf[s][:, BLOCK * (b % 2) : BLOCK * (b % 2 + 1), :]
+                src = banks[b][:].rearrange("p t n -> p n t")
+                if b in VECTOR_RELU:
+                    nc.vector.tensor_scalar_max(dst, src, 0.0)
+                else:
+                    nc.scalar.activation(dst, src, RELU)
 
         def second_layer(s):
             nc.vector.quantize_mx(
@@ -183,24 +183,27 @@ def tile_picked_depth_mlp_relu_srt_p_kernel(
                 MULT,
             )
 
-        hidden(0)
-        hidden(1)
         nc.scalar.copy(
             w2_bf[:].rearrange("p (c i) j -> p c j i", i=PACK),
             w2_raw[:].rearrange("p j (c i) -> p c j i", i=PACK),
         )
-        hidden(2)
+        hidden(0)
+        hidden(1)
         nc.vector.quantize_mx(
             out=w2_codes[:].bitcast(FP8X4),
             scales=w2_scales[:],
             in_=w2_bf[:].rearrange("p n j -> p (n j)"),
         )
         second_layer(0)
+        hidden(2)
+        put_back(0)
+        second_layer(1)
         hidden(3)
-        for s in range(1, SLICES):
-            second_layer(s)
-            put_back(s - 1)
-        put_back(SLICES - 1)
+        put_back(1)
+        second_layer(2)
+        put_back(2)
+        second_layer(3)
+        put_back(3)
 
         nc.sync.dma_start(out[:, 0 : T // 2], out_window[:, 0 : T // 2])
         nc.scalar.dma_start(out[:, T // 2 : T], out_window[:, T // 2 : T])

@@ -23,7 +23,7 @@ SLICE = 256
 BLOCKS = S // BLOCK
 SLICES = S // SLICE
 PER_COL = 16
-VECTOR_RELU = (1,)
+VECTOR_RELU = ()
 
 
 def tile_picked_depth_mlp_relu_srt_p_kernel(
@@ -42,10 +42,12 @@ def tile_picked_depth_mlp_relu_srt_p_kernel(
         scale_window = keep.tile([P, T], U8, name="scale_window", align_bytes=64)
         nc.vector.memset(scale_window[:].bitcast(I32), 0)
         scale_rows = x_scales.bitcast(I32)
-        nc.sync.dma_start(offsets[:], offs)
+        scale_stage = keep.tile([P, T // 4], I32, name="scale_stage")
         for quad in range(4):
             live = slice(32 * quad, 32 * quad + 8)
-            nc.sync.dma_start(scale_window[live, :].bitcast(I32), scale_rows[:, 4 * quad : 4 * quad + 4, :])
+            nc.sync.dma_start(scale_stage[live, :], scale_rows[:, 4 * quad : 4 * quad + 4, :])
+            nc.vector.tensor_copy(scale_window[live, :].bitcast(I32), scale_stage[live, :])
+        nc.sync.dma_start(offsets[:], offs)
         out_window = keep.tile([P, T], F32, name="out_window")
         nc.vector.memset(out_window[:].bitcast(I32), 0)
 
@@ -67,13 +69,13 @@ def tile_picked_depth_mlp_relu_srt_p_kernel(
         load_w1(0, 0)
         load_w1(0, 1)
         load_words(0, 0, reach[1])
-        load_words(0, reach[1], T)
         load_w1(1, 0)
         load_w1(1, 1)
         load_words(1, 0, reach[0])
         w2_raw = keep.tile([P, PACK, N], F32, name="w2_raw")
         nc.sync.dma_start(w2_raw[:], w2.rearrange("(p j) n -> p j n", j=PACK))
         load_words(1, reach[0], reach[1])
+        load_words(0, reach[1], T)
         load_words(1, reach[1], reach[2])
         load_words(1, reach[2], reach[3])
         gate_sb = [keep.tile([P, S // 2], F32, name="gate_sb%d" % g) for g in range(2)]
@@ -108,7 +110,6 @@ def tile_picked_depth_mlp_relu_srt_p_kernel(
         round_w1(0, 1, nc.scalar.copy)
         quantise_w1(0)
         pick0(0)
-        pick0(1)
         round_w1(1, 0, nc.scalar.copy)
         round_w1(1, 1, nc.scalar.copy, 0, 24)
         round_w1(1, 1, nc.vector.tensor_copy, 24, 64)
@@ -189,6 +190,7 @@ def tile_picked_depth_mlp_relu_srt_p_kernel(
         )
         hidden(0)
         hidden(1)
+        pick0(1)
         nc.vector.quantize_mx(
             out=w2_codes[:].bitcast(FP8X4),
             scales=w2_scales[:],

from contextlib import ExitStack

import concourse.mybir as mybir

K, T, S, H, N = 1024, 2048, 1024, 512, 128
FLOPS = 2 * K * H * S + 2 * H * N * S

F32 = mybir.dt.float32
BF16 = mybir.dt.bfloat16
I32 = mybir.dt.int32
U32 = mybir.dt.uint32
U16 = mybir.dt.uint16
U8 = mybir.dt.uint8
FP8X4 = mybir.dt.float8_e4m3fn_x4
RELU = mybir.ActivationFunctionType.Relu
MULT = mybir.AluOpType.mult

P = 128
PACK = 4
PASSES = K // (P * PACK)
BLOCK = 128
SLICE = 256
BLOCKS = S // BLOCK
SLICES = S // SLICE
PER_COL = 16
VECTOR_RELU = ()


def tile_picked_depth_mlp_relu_srt_p_kernel(
    tc, x_words, x_scales, w1, w2, gate, offs, out
):
    nc = tc.nc
    with ExitStack() as ctx:
        keep = ctx.enter_context(tc.tile_pool(name="keep", bufs=1))
        psum = ctx.enter_context(tc.psum_pool(name="psum", bufs=1))

        offsets = keep.tile([P, S // PER_COL], U16, name="offsets")

        def entries(first, count):
            return offsets[:, first // PER_COL : (first + count) // PER_COL]

        scale_window = keep.tile([P, T], U8, name="scale_window", align_bytes=64)
        nc.vector.memset(scale_window[:].bitcast(I32), 0)
        scale_rows = x_scales.bitcast(I32)
        scale_stage = keep.tile([P, T // 4], I32, name="scale_stage")
        for quad in range(4):
            live = slice(32 * quad, 32 * quad + 8)
            nc.sync.dma_start(scale_stage[live, :], scale_rows[:, 4 * quad : 4 * quad + 4, :])
            nc.vector.tensor_copy(scale_window[live, :].bitcast(I32), scale_stage[live, :])
        nc.sync.dma_start(offsets[:], offs)
        out_window = keep.tile([P, T], F32, name="out_window")
        nc.vector.memset(out_window[:].bitcast(I32), 0)

        word_window = [keep.tile([P, T], I32, name="word_window%d" % o) for o in range(PASSES)]

        def load_words(o, first, last):
            src = x_words[o].rearrange("p n t -> p (n t)")[:, PACK * first : PACK * last]
            nc.sync.dma_start(word_window[o][:, first:last], src.bitcast(I32))

        w1_raw = {}

        def load_w1(o, half):
            raw = keep.tile([P, PACK, H // 2], F32, name="w1_raw%d%d" % (o, half))
            rows = w1[512 * o : 512 * (o + 1), (H // 2) * half : (H // 2) * (half + 1)]
            nc.sync.dma_start(raw[:], rows.rearrange("(p j) c -> p j c", j=PACK))
            w1_raw[o, half] = raw

        reach = [T - S + SLICE * (s + 1) for s in range(SLICES)]
        load_w1(0, 0)
        load_w1(0, 1)
        load_words(0, 0, reach[1])
        load_w1(1, 0)
        load_w1(1, 1)
        load_words(1, 0, reach[0])
        w2_raw = keep.tile([P, PACK, N], F32, name="w2_raw")
        nc.sync.dma_start(w2_raw[:], w2.rearrange("(p j) n -> p j n", j=PACK))
        load_words(1, reach[0], reach[1])
        load_words(0, reach[1], T)
        load_words(1, reach[1], reach[2])
        load_words(1, reach[2], reach[3])
        gate_sb = [keep.tile([P, S // 2], F32, name="gate_sb%d" % g) for g in range(2)]
        for g in range(2):
            nc.sync.dma_start(gate_sb[g][:], gate[:, (S // 2) * g : (S // 2) * (g + 1)])

        picked_scales = keep.tile([P, S], U8, name="picked_scales", align_bytes=64)
        nc.vector.tensor_copy(picked_scales[:], scale_window[:].indirect(offsets[:]))
        picked0 = [keep.tile([P, S // 2], U32, name="picked0_%d" % g, align_bytes=64) for g in range(2)]

        def pick0(g):
            window = word_window[0][:, 0 : reach[2 * g + 1]].bitcast(U32)
            nc.vector.tensor_copy(picked0[g][:], window.indirect(entries((S // 2) * g, S // 2)))

        w1_bf = [keep.tile([P, PACK, P, PACK], BF16, name="w1_bf%d" % o, align_bytes=64) for o in range(PASSES)]
        w1_codes = [keep.tile([P, H], U32, name="w1_codes%d" % o, align_bytes=64) for o in range(PASSES)]
        w1_scales = [keep.tile([P, H], U8, name="w1_scales%d" % o, align_bytes=64) for o in range(PASSES)]

        def round_w1(o, half, copy, first=0, last=64):
            dst = w1_bf[o][:, :, 64 * half + first : 64 * half + last, :].rearrange("p t m j -> p m j t")
            src = w1_raw[o, half][:, :, PACK * first : PACK * last]
            copy(dst, src.rearrange("p j (m t) -> p m j t", t=PACK))

        def quantise_w1(o):
            nc.vector.quantize_mx(
                out=w1_codes[o][:].bitcast(FP8X4),
                scales=w1_scales[o][:],
                in_=w1_bf[o][:].rearrange("p t m j -> p (t m j)"),
            )

        round_w1(0, 0, nc.scalar.copy)
        round_w1(0, 1, nc.scalar.copy)
        quantise_w1(0)
        pick0(0)
        round_w1(1, 0, nc.scalar.copy)
        round_w1(1, 1, nc.scalar.copy, 0, 24)
        round_w1(1, 1, nc.vector.tensor_copy, 24, 64)
        quantise_w1(1)

        banks = {}
        picked1 = [keep.tile([P, SLICE], U32, name="picked1_%d" % s, align_bytes=64) for s in range(SLICES)]

        def first_layer(o, b):
            if o == 0:
                words = picked0[b // 4][:, BLOCK * (b % 4) : BLOCK * (b % 4 + 1)]
            else:
                words = picked1[b // 2][:, BLOCK * (b % 2) : BLOCK * (b % 2 + 1)]
            for t in range(PACK):
                nc.tensor.matmul_mx(
                    out=banks[b][:, t, :],
                    lhsT=w1_codes[o][:, P * t : P * (t + 1)].bitcast(FP8X4),
                    lhsT_scale=w1_scales[o][:, P * t : P * (t + 1)],
                    rhs=words.bitcast(FP8X4),
                    rhs_scale=picked_scales[4 * o : P, BLOCK * b : BLOCK * (b + 1)],
                    start=(o == 0 and t == 0),
                    stop=(o == PASSES - 1 and t == PACK - 1),
                )

        w2_bf = keep.tile([P, N, PACK], BF16, name="w2_bf", align_bytes=64)
        w2_codes = keep.tile([P, N], U32, name="w2_codes", align_bytes=64)
        w2_scales = keep.tile([P, N], U8, name="w2_scales", align_bytes=64)

        h_bf = [keep.tile([P, SLICE, PACK], BF16, name="h_bf%d" % s, align_bytes=64) for s in range(SLICES)]
        h_codes = [keep.tile([P, SLICE], U32, name="h_codes%d" % s, align_bytes=64) for s in range(SLICES)]
        h_scales = [keep.tile([P, SLICE], U8, name="h_scales%d" % s, align_bytes=64) for s in range(SLICES)]
        y_sb = [keep.tile([P, SLICE], F32, name="y_sb%d" % s) for s in range(SLICES)]

        def hidden(s):
            nc.vector.tensor_copy(
                picked1[s][:], word_window[1][:, 0 : reach[s]].bitcast(U32).indirect(entries(SLICE * s, SLICE))
            )
            for b in (2 * s, 2 * s + 1):
                banks[b] = psum.tile([P, PACK, BLOCK], F32, name="bank%d" % b, tag="bank%d" % (b % 4))
                first_layer(0, b)
                first_layer(1, b)
                dst = h_bf[s][:, BLOCK * (b % 2) : BLOCK * (b % 2 + 1), :]
                src = banks[b][:].rearrange("p t n -> p n t")
                if b in VECTOR_RELU:
                    nc.vector.tensor_scalar_max(dst, src, 0.0)
                else:
                    nc.scalar.activation(dst, src, RELU)

        def second_layer(s):
            nc.vector.quantize_mx(
                out=h_codes[s][:].bitcast(FP8X4),
                scales=h_scales[s][:],
                in_=h_bf[s][:].rearrange("p n t -> p (n t)"),
            )
            y_bank = psum.tile([P, SLICE], F32, name="y_bank%d" % s, tag="y_bank%d" % s)
            nc.tensor.matmul_mx(
                out=y_bank[:],
                lhsT=w2_codes[:].bitcast(FP8X4),
                lhsT_scale=w2_scales[:],
                rhs=h_codes[s][:].bitcast(FP8X4),
                rhs_scale=h_scales[s][:],
                start=True,
                stop=True,
            )
            nc.scalar.copy(y_sb[s][:], y_bank[:])

        def put_back(s):
            nc.vector.tensor_tensor(
                out_window[:].indirect(entries(SLICE * s, SLICE)),
                y_sb[s][:],
                gate_sb[s // 2][:, SLICE * (s % 2) : SLICE * (s % 2 + 1)],
                MULT,
            )

        nc.scalar.copy(
            w2_bf[:].rearrange("p (c i) j -> p c j i", i=PACK),
            w2_raw[:].rearrange("p j (c i) -> p c j i", i=PACK),
        )
        hidden(0)
        hidden(1)
        pick0(1)
        nc.vector.quantize_mx(
            out=w2_codes[:].bitcast(FP8X4),
            scales=w2_scales[:],
            in_=w2_bf[:].rearrange("p n j -> p (n j)"),
        )
        second_layer(0)
        hidden(2)
        put_back(0)
        second_layer(1)
        hidden(3)
        put_back(1)
        second_layer(2)
        put_back(2)
        second_layer(3)
        put_back(3)

        nc.sync.dma_start(out[:, 0 : T // 2], out_window[:, 0 : T // 2])
        nc.scalar.dma_start(out[:, T // 2 : T], out_window[:, T // 2 : T])
